import numpy as np
import ml_dtypes


def mxq(x, axis, fmt="e4m3"):
    dtype, down = {"e4m3": (ml_dtypes.float8_e4m3fn, 7), "e5m2": (ml_dtypes.float8_e5m2, 14)}[fmt]
    v = np.moveaxis(np.asarray(x, np.float32).astype(ml_dtypes.bfloat16).astype(np.float64), axis, -1)
    blocks = v.reshape(v.shape[:-1] + (-1, 32))
    amax = np.abs(blocks).max(-1, keepdims=True)
    byte = np.maximum(np.where(amax > 0, np.frexp(amax)[1] - 1 + 127, 0) - down, 1)
    scale = np.exp2(byte - 127.0)
    codes = (blocks / scale).astype(np.float32).astype(dtype).astype(np.float64)
    return np.moveaxis((codes * scale).reshape(v.shape), -1, axis)


WIDE = False


def mx_kscale(k):
    if not WIDE:
        return np.ones(k)
    levels = np.array([10, -10, 5, -5, 0])
    if k % 512:
        return np.exp2(np.random.permutation(np.resize(levels, k // 32))).repeat(32)
    a = np.empty((k // 512, 16))
    for p in range(k // 512):
        a[p, :8] = np.random.permutation(np.resize(levels, 8))
        for g in range(8):
            far = levels[np.abs(levels - a[p, g]) >= 10]
            a[p, g + 8] = far[np.random.randint(len(far))]
    return np.exp2(a.ravel()).repeat(32)


def f64(x):
    return np.asarray(x).astype(np.float64)


def striped(idx):
    return np.tile(idx.reshape(-1, 16).T, (8, 1)).astype(np.uint16)


def unstriped(offs):
    return offs[:16].T.reshape(-1).astype(np.int64)


def pack_weight(w):
    k, n = w.shape
    w = f64(np.asarray(w, np.float32).astype(ml_dtypes.bfloat16)).reshape(k // 32, 32, n)
    amax = np.abs(w).max(1)
    byte = np.clip(np.where(amax > 0, np.frexp(amax)[1] - 1 + 127 - 7, 1), 1, 254)
    scaled = (w * np.exp2(127.0 - byte)[:, None, :]).reshape(k, n).astype(np.float32)
    words = np.ascontiguousarray(scaled.reshape(k // 512, 128, 4, n).transpose(0, 1, 3, 2)).astype(ml_dtypes.float8_e4m3fn).view(np.uint8)
    return words, np.ascontiguousarray(byte.astype(np.uint8).reshape(k // 512, 16, n))


def unpack_weight(words, scales):
    g, p, n, _ = words.shape
    vals = np.ascontiguousarray(words).view(ml_dtypes.float8_e4m3fn).astype(np.float64) * np.repeat(np.exp2(scales.astype(np.float64) - 127.0), 8, axis=1)[..., None]
    return vals.transpose(0, 1, 3, 2).reshape(g * 512, n)


def planes(y):
    n, m = y.shape
    v = y.astype(np.float32).astype(ml_dtypes.bfloat16).astype(np.float64).reshape(n // 32, 32, m)
    top = np.abs(v).max(1)
    byte = np.clip(np.where(top > 0, np.frexp(top)[1] - 1 + 127 - 7, 1), 1, 254)
    codes = (v * np.exp2(127.0 - byte)[:, None, :]).reshape(n, m).astype(np.float32).astype(ml_dtypes.float8_e4m3fn).view(np.uint8)
    words = codes.reshape(n // 512, 128, 4, m).transpose(0, 1, 3, 2)
    return np.ascontiguousarray(words), np.ascontiguousarray(byte.astype(np.uint8).reshape(n // 512, 16, m))


def relu(v):
    return np.maximum(v, 0.0)


K, T, S, V, H, N = 512, 2048, 1536, 512, 512, 512


def setup_inputs():
    n = np.random.standard_normal
    s = mx_kscale(K)[:, None]
    u = mx_kscale(H)
    packed_xT = pack_weight(n((K, T)) * s)
    return {
        "x_words": packed_xT[0],
        "x_scales": packed_xT[1],
        "w1": (n((K, H)) / np.sqrt(K) / s * u).astype(np.float32),
        "w2": (n((K, N)) / np.sqrt(K) / s).astype(np.float32),
        "w3": (n((H, N)) / np.sqrt(H) / u[:, None]).astype(np.float32),
        "offs": striped(np.random.permutation(T)[:S]),
    }


def reference(x_words, x_scales, w1, w2, w3, offs):
    xq = unpack_weight(x_words, x_scales)[:, unstriped(offs)]
    w1q = mxq(f64(w1), 0, "e4m3")
    h0 = w1q.T @ xq[:, :V]
    w2q = mxq(f64(w2), 0, "e4m3")
    e1 = w2q.T @ xq[:, V:2 * V]
    e2 = w2q.T @ xq[:, 2 * V:3 * V]
    h1 = w1q.T @ xq[:, V:2 * V]
    z = h0 * e1 + h0 * e2 + h1 * e2
    out_0 = relu(mxq(f64(w3), 0, "e4m3").T @ mxq(z, 0, "e4m3"))
    return (out_0,) + planes(out_0)

@@ -1,0 +1,195 @@
+from contextlib import ExitStack
+
+import concourse.mybir as mybir
+
+K, T, V, H, N = 512, 2048, 512, 512, 512
+FIELDS = 3
+FLOPS = 5 * 2 * 512 * 512 * 512
+
+F32 = mybir.dt.float32
+BF16 = mybir.dt.bfloat16
+I32 = mybir.dt.int32
+U32 = mybir.dt.uint32
+U16 = mybir.dt.uint16
+U8 = mybir.dt.uint8
+FP8X4 = mybir.dt.float8_e4m3fn_x4
+MULT = mybir.AluOpType.mult
+ADD = mybir.AluOpType.add
+RELU = mybir.ActivationFunctionType.Relu
+
+P = 128
+PACK = 4
+CHUNK = 128
+CHUNKS = V // CHUNK
+GATHER = 256
+PER_COL = 16
+
+
+def tile_picked_zfibi_relu_po_kernel(tc, x_words, x_scales, w1, w2, w3, offs, out_0, out_1, out_2):
+    nc = tc.nc
+    with ExitStack() as ctx:
+        keep = ctx.enter_context(tc.tile_pool(name="keep", bufs=1))
+        ring = ctx.enter_context(tc.tile_pool(name="ring", bufs=4))
+        psum = ctx.enter_context(tc.psum_pool(name="psum", bufs=1))
+
+        offsets = keep.tile([P, FIELDS * V // PER_COL], U16, name="offsets")
+        nc.sync.dma_start(offsets[:], offs)
+
+        scale_table = keep.tile([P, T], U8, name="scale_table", align_bytes=64)
+        nc.vector.memset(scale_table[:].bitcast(I32), 0)
+        warm = keep.tile([P, 2], F32, name="warm")
+        nc.vector.memset(warm[:, 0:1], 0.0)
+        nc.scalar.activation(out=warm[:, 1:2], in_=warm[:, 0:1], func=RELU)
+
+        def load_part(w, name, part, parts):
+            width = w.shape[1] // parts
+            raw = keep.tile([P, PACK, width], F32, name="%s_raw%d" % (name, part), tag="%s_raw%d" % (name, part))
+            nc.sync.dma_start(raw[:], w[:, part * width : (part + 1) * width].rearrange("(p j) c -> p j c", j=PACK))
+            return raw
+
+        def load_weight(w, name, parts):
+            return [load_part(w, name, part, parts) for part in range(parts)]
+
+        w1_raw = [load_part(w1, "w1", 0, 2)]
+        for q in range(4):
+            nc.sync.dma_start(
+                scale_table[32 * q : 32 * q + 4, :].bitcast(I32), x_scales[0, 4 * q : 4 * q + 4, :].bitcast(I32)
+            )
+        w1_raw.append(load_part(w1, "w1", 1, 2))
+        word_table = keep.tile([P, T], U32, name="word_table", align_bytes=64)
+        nc.sync.dma_start(word_table[:].bitcast(I32), x_words[0].rearrange("p c r -> p (c r)").bitcast(I32))
+        w2_raw = load_weight(w2, "w2", 2)
+        w3_raw = load_weight(w3, "w3", 2)
+
+        def round_weight(raws, name):
+            grouped = keep.tile([P, PACK * P * PACK], BF16, name=name + "_grouped", tag=name + "_grouped", align_bytes=64)
+            dealt = grouped[:].rearrange("p (t m j) -> p m t j", t=PACK, j=PACK)
+            step = P // len(raws)
+            for part, raw in enumerate(raws):
+                nc.scalar.copy(
+                    out=dealt[:, part * step : (part + 1) * step], in_=raw[:].rearrange("p j (m t) -> p m t j", t=PACK)
+                )
+            return grouped
+
+        def quantise(grouped, codes, scales):
+            nc.vector.quantize_mx(out=codes.bitcast(FP8X4), scales=scales, in_=grouped)
+
+        def quantise_weight(grouped, name):
+            codes = keep.tile([P, PACK * P], U32, name=name + "_codes", align_bytes=64)
+            scales = keep.tile([P, PACK * P], U8, name=name + "_scales", align_bytes=64)
+            quantise(grouped[:], codes[:], scales[:])
+            return codes, scales
+
+        picked_scales = keep.tile([P, FIELDS * V], U8, name="picked_scales", align_bytes=64)
+        nc.vector.tensor_copy(picked_scales[:], scale_table[:].indirect(offsets[:]))
+
+        picked_words = {}
+
+        def gather_words(field, half, tag=None):
+            name = "picked_words%d%d" % (field, half)
+            words = keep.tile([P, GATHER], U32, name=name, tag=tag or name, align_bytes=64)
+            first = (field * V + half * GATHER) // PER_COL
+            nc.vector.tensor_copy(words[:], word_table[:].indirect(offsets[:, first : first + GATHER // PER_COL]))
+            picked_words[(field, half)] = words
+
+        def picked(field, c):
+            half, start = divmod(c * CHUNK, GATHER)
+            first = field * V + c * CHUNK
+            return picked_words[(field, half)][:, start : start + CHUNK], picked_scales[:, first : first + CHUNK]
+
+        def product(weight, movings, tag, bufs):
+            codes, scales = weight
+            bank = psum.tile([P, PACK, CHUNK], F32, name="bank", tag=tag, bufs=bufs)
+            for t in range(PACK):
+                cols = slice(t * P, (t + 1) * P)
+                for n, (words, word_scales) in enumerate(movings):
+                    nc.tensor.matmul_mx(
+                        out=bank[:, t, :],
+                        lhsT=codes[:, cols].bitcast(FP8X4),
+                        lhsT_scale=scales[:, cols],
+                        rhs=words.bitcast(FP8X4),
+                        rhs_scale=word_scales,
+                        start=(n == 0),
+                        stop=(n == len(movings) - 1),
+                    )
+            return bank
+
+        def woven(bank):
+            return bank[:].rearrange("p t v -> p v t")
+
+        left = {}
+
+        def left_products(c):
+            for field in (1, 0):
+                bank = product(w1_q, [picked(field, c)], "outer", 5)
+                tag = "w2_raw%d" % (1 - field) if c == 0 else "h%d%d" % (field, c)
+                h = keep.tile([P, CHUNK, PACK], F32, name="h%d%d" % (field, c), tag=tag)
+                nc.scalar.copy(out=h[:], in_=woven(bank))
+                left[(field, c)] = h
+
+        z_q = {}
+
+        def interact(c):
+            e2 = product(w2_q, [picked(2, c)], "right", 3)
+            e12 = product(w2_q, [picked(1, c), picked(2, c)], "right", 3)
+            term_b = ring.tile([P, CHUNK, PACK], F32, name="term_b")
+            nc.vector.tensor_tensor(term_b[:], woven(e2), left[(1, c)][:], MULT)
+            term_a = ring.tile([P, CHUNK, PACK], F32, name="term_a")
+            nc.vector.tensor_tensor(term_a[:], woven(e12), left[(0, c)][:], MULT)
+            z = ring.tile([P, CHUNK, PACK], BF16, name="z", align_bytes=64)
+            nc.vector.tensor_tensor(z[:], term_a[:], term_b[:], ADD)
+            z_q[c] = z
+
+        y_codes = keep.tile([P, V], U32, name="y_codes", align_bytes=64)
+        y_scales = keep.tile([P, V], U8, name="y_scales", align_bytes=64)
+        out_rows = out_0.rearrange("(p t) v -> p t v", t=PACK)
+        out_words = out_1[0].rearrange("p c r -> p (c r)").bitcast(I32)
+        y_round = {}
+
+        def last_layer(c):
+            z_codes = ring.tile([P, CHUNK], U32, name="z_codes", align_bytes=64)
+            z_scales = ring.tile([P, CHUNK], U8, name="z_scales", align_bytes=64)
+            quantise(z_q[c][:].rearrange("p v t -> p (v t)"), z_codes[:], z_scales[:])
+            bank = product(w3_q, [(z_codes[:], z_scales[:])], "outer", 5)
+            y = keep.tile([P, PACK, CHUNK], F32, name="y%d" % c)
+            nc.scalar.activation(out=y[:], in_=bank[:], func=RELU)
+            nc.sync.dma_start(out_rows[:, :, c * CHUNK : (c + 1) * CHUNK], y[:])
+            rounded = ring.tile([P, CHUNK, PACK], BF16, name="rounded", align_bytes=64)
+            if c < CHUNKS - 1:
+                nc.scalar.activation(out=rounded[:], in_=woven(bank), func=RELU)
+            else:
+                nc.vector.tensor_copy(rounded[:], woven(y))
+            y_round[c] = rounded
+
+        def planes(c):
+            cols = slice(c * CHUNK, (c + 1) * CHUNK)
+            quantise(y_round[c][:].rearrange("p v t -> p (v t)"), y_codes[:, cols], y_scales[:, cols])
+            nc.sync.dma_start(out_words[:, cols], y_codes[:, cols].bitcast(I32))
+
+        w1_grouped = round_weight(w1_raw, "w1")
+        gather_words(1, 0)
+        gather_words(0, 0)
+        w1_q = quantise_weight(w1_grouped, "w1")
+        w2_grouped = round_weight(w2_raw, "w2")
+        gather_words(2, 0)
+        gather_words(1, 1)
+        gather_words(0, 1)
+        w2_q = quantise_weight(w2_grouped, "w2")
+        left_products(0)
+        gather_words(2, 1, tag="w2_grouped")
+        left_products(1)
+        interact(0)
+        w3_grouped = round_weight(w3_raw, "w3")
+        left_products(2)
+        w3_q = quantise_weight(w3_grouped, "w3")
+        interact(1)
+        left_products(3)
+        for c in range(CHUNKS):
+            last_layer(c)
+            if c + 2 < CHUNKS:
+                interact(c + 2)
+            planes(c)
+        for q in range(4):
+            nc.scalar.dma_start(
+                out_2[0, 4 * q : 4 * q + 4, :].bitcast(I32), y_scales[32 * q : 32 * q + 4, :].bitcast(I32)
+            )

@@ -23,6 +23,8 @@ CHUNK = 128
 CHUNKS = V // CHUNK
 GATHER = 256
 PER_COL = 16
+FIRST = 512
+SCALAR_ROUNDS = 2
 
 
 def tile_picked_zfibi_relu_po_kernel(tc, x_words, x_scales, w1, w2, w3, offs, out_0, out_1, out_2):
@@ -50,25 +52,28 @@ def tile_picked_zfibi_relu_po_kernel(tc, x_words, x_scales, w1, w2, w3, offs, ou
         def load_weight(w, name, parts):
             return [load_part(w, name, part, parts) for part in range(parts)]
 
-        w1_raw = [load_part(w1, "w1", 0, 2)]
+        word_table = keep.tile([P, T], U32, name="word_table", align_bytes=64)
+        table_words = x_words[0].rearrange("p c r -> p (c r)").bitcast(I32)
+        nc.sync.dma_start(word_table[:, :FIRST].bitcast(I32), table_words[:, :FIRST])
         for q in range(4):
             nc.sync.dma_start(
                 scale_table[32 * q : 32 * q + 4, :].bitcast(I32), x_scales[0, 4 * q : 4 * q + 4, :].bitcast(I32)
             )
-        w1_raw.append(load_part(w1, "w1", 1, 2))
-        word_table = keep.tile([P, T], U32, name="word_table", align_bytes=64)
-        nc.sync.dma_start(word_table[:].bitcast(I32), x_words[0].rearrange("p c r -> p (c r)").bitcast(I32))
+        w1_raw = load_weight(w1, "w1", 1)
+        nc.sync.dma_start(word_table[:, FIRST:].bitcast(I32), table_words[:, FIRST:])
         w2_raw = load_weight(w2, "w2", 2)
-        w3_raw = load_weight(w3, "w3", 2)
+        w3_raw = load_weight(w3, "w3", 1)
 
         def round_weight(raws, name):
             grouped = keep.tile([P, PACK * P * PACK], BF16, name=name + "_grouped", tag=name + "_grouped", align_bytes=64)
-            dealt = grouped[:].rearrange("p (t m j) -> p m t j", t=PACK, j=PACK)
-            step = P // len(raws)
-            for part, raw in enumerate(raws):
-                nc.scalar.copy(
-                    out=dealt[:, part * step : (part + 1) * step], in_=raw[:].rearrange("p j (m t) -> p m t j", t=PACK)
-                )
+            dealt = grouped[:].rearrange("p (t m j) -> p m j t", t=PACK, j=PACK)
+            step = P // 2
+            for part in range(2):
+                if len(raws) == 2:
+                    source = raws[part][:].rearrange("p j (m t) -> p m j t", t=PACK)
+                else:
+                    source = raws[0][:].rearrange("p j (m t) -> p m j t", t=PACK)[:, part * step : (part + 1) * step]
+                nc.scalar.copy(out=dealt[:, part * step : (part + 1) * step], in_=source)
             return grouped
 
         def quantise(grouped, codes, scales):
@@ -85,12 +90,13 @@ def tile_picked_zfibi_relu_po_kernel(tc, x_words, x_scales, w1, w2, w3, offs, ou
 
         picked_words = {}
 
-        def gather_words(field, half, tag=None):
-            name = "picked_words%d%d" % (field, half)
-            words = keep.tile([P, GATHER], U32, name=name, tag=tag or name, align_bytes=64)
-            first = (field * V + half * GATHER) // PER_COL
-            nc.vector.tensor_copy(words[:], word_table[:].indirect(offsets[:, first : first + GATHER // PER_COL]))
-            picked_words[(field, half)] = words
+        def gather_words(pieces, tag):
+            words = keep.tile([P, len(pieces) * GATHER], U32, name="picked_words", tag=tag, align_bytes=64)
+            for n, (field, half) in enumerate(pieces):
+                first = (field * V + half * GATHER) // PER_COL
+                piece = words[:, n * GATHER : (n + 1) * GATHER]
+                nc.vector.tensor_copy(piece, word_table[:].indirect(offsets[:, first : first + GATHER // PER_COL]))
+                picked_words[(field, half)] = piece
 
         def picked(field, c):
             half, start = divmod(c * CHUNK, GATHER)
@@ -120,12 +126,11 @@ def tile_picked_zfibi_relu_po_kernel(tc, x_words, x_scales, w1, w2, w3, offs, ou
         left = {}
 
         def left_products(c):
+            h = keep.tile([P, 2, CHUNK, PACK], F32, name="h", tag="w2_raw%d" % c if c < 2 else "h%d" % c)
             for field in (1, 0):
                 bank = product(w1_q, [picked(field, c)], "outer", 5)
-                tag = "w2_raw%d" % (1 - field) if c == 0 else "h%d%d" % (field, c)
-                h = keep.tile([P, CHUNK, PACK], F32, name="h%d%d" % (field, c), tag=tag)
-                nc.scalar.copy(out=h[:], in_=woven(bank))
-                left[(field, c)] = h
+                nc.scalar.copy(out=h[:, field], in_=woven(bank))
+                left[(field, c)] = h[:, field]
 
         z_q = {}
 
@@ -133,9 +138,9 @@ def tile_picked_zfibi_relu_po_kernel(tc, x_words, x_scales, w1, w2, w3, offs, ou
             e2 = product(w2_q, [picked(2, c)], "right", 3)
             e12 = product(w2_q, [picked(1, c), picked(2, c)], "right", 3)
             term_b = ring.tile([P, CHUNK, PACK], F32, name="term_b")
-            nc.vector.tensor_tensor(term_b[:], woven(e2), left[(1, c)][:], MULT)
+            nc.vector.tensor_tensor(term_b[:], woven(e2), left[(1, c)], MULT)
             term_a = ring.tile([P, CHUNK, PACK], F32, name="term_a")
-            nc.vector.tensor_tensor(term_a[:], woven(e12), left[(0, c)][:], MULT)
+            nc.vector.tensor_tensor(term_a[:], woven(e12), left[(0, c)], MULT)
             z = ring.tile([P, CHUNK, PACK], BF16, name="z", align_bytes=64)
             nc.vector.tensor_tensor(z[:], term_a[:], term_b[:], ADD)
             z_q[c] = z
@@ -153,34 +158,37 @@ def tile_picked_zfibi_relu_po_kernel(tc, x_words, x_scales, w1, w2, w3, offs, ou
             bank = product(w3_q, [(z_codes[:], z_scales[:])], "outer", 5)
             y = keep.tile([P, PACK, CHUNK], F32, name="y%d" % c)
             nc.scalar.activation(out=y[:], in_=bank[:], func=RELU)
-            nc.sync.dma_start(out_rows[:, :, c * CHUNK : (c + 1) * CHUNK], y[:])
-            rounded = ring.tile([P, CHUNK, PACK], BF16, name="rounded", align_bytes=64)
-            if c < CHUNKS - 1:
-                nc.scalar.activation(out=rounded[:], in_=woven(bank), func=RELU)
-            else:
-                nc.vector.tensor_copy(rounded[:], woven(y))
-            y_round[c] = rounded
+            queue = nc.scalar if c == CHUNKS - 1 else nc.sync
+            queue.dma_start(out_rows[:, :, c * CHUNK : (c + 1) * CHUNK], y[:])
+            y_round[c] = (bank, y)
 
         def planes(c):
             cols = slice(c * CHUNK, (c + 1) * CHUNK)
-            quantise(y_round[c][:].rearrange("p v t -> p (v t)"), y_codes[:, cols], y_scales[:, cols])
-            nc.sync.dma_start(out_words[:, cols], y_codes[:, cols].bitcast(I32))
+            bank, y = y_round[c]
+            rounded = ring.tile([P, CHUNK, PACK], BF16, name="rounded", align_bytes=64)
+            if c < SCALAR_ROUNDS:
+                nc.scalar.activation(out=rounded[:], in_=woven(bank), func=RELU)
+            else:
+                nc.vector.tensor_copy(
+                    rounded[:].rearrange("p (u i) t -> p u t i", i=4), y[:].rearrange("p t (u i) -> p u t i", i=4)
+                )
+            quantise(rounded[:].rearrange("p v t -> p (v t)"), y_codes[:, cols], y_scales[:, cols])
+            if c % 2 == 1:
+                pair = slice((c - 1) * CHUNK, (c + 1) * CHUNK)
+                nc.sync.dma_start(out_words[:, pair], y_codes[:, pair].bitcast(I32))
 
         w1_grouped = round_weight(w1_raw, "w1")
-        gather_words(1, 0)
-        gather_words(0, 0)
+        gather_words([(1, 0), (0, 0)], "first_words")
         w1_q = quantise_weight(w1_grouped, "w1")
         w2_grouped = round_weight(w2_raw, "w2")
-        gather_words(2, 0)
-        gather_words(1, 1)
-        gather_words(0, 1)
+        gather_words([(2, 0), (1, 1), (0, 1)], "w1_grouped")
         w2_q = quantise_weight(w2_grouped, "w2")
         left_products(0)
-        gather_words(2, 1, tag="w2_grouped")
+        gather_words([(2, 1)], "w2_grouped")
         left_products(1)
         interact(0)
-        w3_grouped = round_weight(w3_raw, "w3")
         left_products(2)
+        w3_grouped = round_weight(w3_raw, "w3")
         w3_q = quantise_weight(w3_grouped, "w3")
         interact(1)
         left_products(3)
@@ -188,8 +196,10 @@ def tile_picked_zfibi_relu_po_kernel(tc, x_words, x_scales, w1, w2, w3, offs, ou
             last_layer(c)
             if c + 2 < CHUNKS:
                 interact(c + 2)
+        for c in range(CHUNKS):
             planes(c)
         for q in range(4):
-            nc.scalar.dma_start(
+            queue = nc.scalar if q % 2 else nc.sync
+            queue.dma_start(
                 out_2[0, 4 * q : 4 * q + 4, :].bitcast(I32), y_scales[32 * q : 32 * q + 4, :].bitcast(I32)
             )

from contextlib import ExitStack

import concourse.mybir as mybir

K, T, V, H, N = 512, 2048, 512, 512, 512
FIELDS = 3
FLOPS = 5 * 2 * 512 * 512 * 512

F32 = mybir.dt.float32
BF16 = mybir.dt.bfloat16
I32 = mybir.dt.int32
U32 = mybir.dt.uint32
U16 = mybir.dt.uint16
U8 = mybir.dt.uint8
FP8X4 = mybir.dt.float8_e4m3fn_x4
MULT = mybir.AluOpType.mult
ADD = mybir.AluOpType.add
RELU = mybir.ActivationFunctionType.Relu

P = 128
PACK = 4
CHUNK = 128
CHUNKS = V // CHUNK
GATHER = 256
PER_COL = 16
FIRST = 512
SCALAR_ROUNDS = 2


def tile_picked_zfibi_relu_po_kernel(tc, x_words, x_scales, w1, w2, w3, offs, out_0, out_1, out_2):
    nc = tc.nc
    with ExitStack() as ctx:
        keep = ctx.enter_context(tc.tile_pool(name="keep", bufs=1))
        ring = ctx.enter_context(tc.tile_pool(name="ring", bufs=4))
        psum = ctx.enter_context(tc.psum_pool(name="psum", bufs=1))

        offsets = keep.tile([P, FIELDS * V // PER_COL], U16, name="offsets")
        nc.sync.dma_start(offsets[:], offs)

        scale_table = keep.tile([P, T], U8, name="scale_table", align_bytes=64)
        nc.vector.memset(scale_table[:].bitcast(I32), 0)
        warm = keep.tile([P, 2], F32, name="warm")
        nc.vector.memset(warm[:, 0:1], 0.0)
        nc.scalar.activation(out=warm[:, 1:2], in_=warm[:, 0:1], func=RELU)

        def load_part(w, name, part, parts):
            width = w.shape[1] // parts
            raw = keep.tile([P, PACK, width], F32, name="%s_raw%d" % (name, part), tag="%s_raw%d" % (name, part))
            nc.sync.dma_start(raw[:], w[:, part * width : (part + 1) * width].rearrange("(p j) c -> p j c", j=PACK))
            return raw

        def load_weight(w, name, parts):
            return [load_part(w, name, part, parts) for part in range(parts)]

        word_table = keep.tile([P, T], U32, name="word_table", align_bytes=64)
        table_words = x_words[0].rearrange("p c r -> p (c r)").bitcast(I32)
        nc.sync.dma_start(word_table[:, :FIRST].bitcast(I32), table_words[:, :FIRST])
        for q in range(4):
            nc.sync.dma_start(
                scale_table[32 * q : 32 * q + 4, :].bitcast(I32), x_scales[0, 4 * q : 4 * q + 4, :].bitcast(I32)
            )
        w1_raw = load_weight(w1, "w1", 1)
        nc.sync.dma_start(word_table[:, FIRST:].bitcast(I32), table_words[:, FIRST:])
        w2_raw = load_weight(w2, "w2", 2)
        w3_raw = load_weight(w3, "w3", 1)

        def round_weight(raws, name):
            grouped = keep.tile([P, PACK * P * PACK], BF16, name=name + "_grouped", tag=name + "_grouped", align_bytes=64)
            dealt = grouped[:].rearrange("p (t m j) -> p m j t", t=PACK, j=PACK)
            step = P // 2
            for part in range(2):
                if len(raws) == 2:
                    source = raws[part][:].rearrange("p j (m t) -> p m j t", t=PACK)
                else:
                    source = raws[0][:].rearrange("p j (m t) -> p m j t", t=PACK)[:, part * step : (part + 1) * step]
                nc.scalar.copy(out=dealt[:, part * step : (part + 1) * step], in_=source)
            return grouped

        def quantise(grouped, codes, scales):
            nc.vector.quantize_mx(out=codes.bitcast(FP8X4), scales=scales, in_=grouped)

        def quantise_weight(grouped, name):
            codes = keep.tile([P, PACK * P], U32, name=name + "_codes", align_bytes=64)
            scales = keep.tile([P, PACK * P], U8, name=name + "_scales", align_bytes=64)
            quantise(grouped[:], codes[:], scales[:])
            return codes, scales

        picked_scales = keep.tile([P, FIELDS * V], U8, name="picked_scales", align_bytes=64)
        nc.vector.tensor_copy(picked_scales[:], scale_table[:].indirect(offsets[:]))

        picked_words = {}

        def gather_words(pieces, tag):
            words = keep.tile([P, len(pieces) * GATHER], U32, name="picked_words", tag=tag, align_bytes=64)
            for n, (field, half) in enumerate(pieces):
                first = (field * V + half * GATHER) // PER_COL
                piece = words[:, n * GATHER : (n + 1) * GATHER]
                nc.vector.tensor_copy(piece, word_table[:].indirect(offsets[:, first : first + GATHER // PER_COL]))
                picked_words[(field, half)] = piece

        def picked(field, c):
            half, start = divmod(c * CHUNK, GATHER)
            first = field * V + c * CHUNK
            return picked_words[(field, half)][:, start : start + CHUNK], picked_scales[:, first : first + CHUNK]

        def product(weight, movings, tag, bufs):
            codes, scales = weight
            bank = psum.tile([P, PACK, CHUNK], F32, name="bank", tag=tag, bufs=bufs)
            for t in range(PACK):
                cols = slice(t * P, (t + 1) * P)
                for n, (words, word_scales) in enumerate(movings):
                    nc.tensor.matmul_mx(
                        out=bank[:, t, :],
                        lhsT=codes[:, cols].bitcast(FP8X4),
                        lhsT_scale=scales[:, cols],
                        rhs=words.bitcast(FP8X4),
                        rhs_scale=word_scales,
                        start=(n == 0),
                        stop=(n == len(movings) - 1),
                    )
            return bank

        def woven(bank):
            return bank[:].rearrange("p t v -> p v t")

        left = {}

        def left_products(c):
            h = keep.tile([P, 2, CHUNK, PACK], F32, name="h", tag="w2_raw%d" % c if c < 2 else "h%d" % c)
            for field in (1, 0):
                bank = product(w1_q, [picked(field, c)], "outer", 5)
                nc.scalar.copy(out=h[:, field], in_=woven(bank))
                left[(field, c)] = h[:, field]

        z_q = {}

        def interact(c):
            e2 = product(w2_q, [picked(2, c)], "right", 3)
            e12 = product(w2_q, [picked(1, c), picked(2, c)], "right", 3)
            term_b = ring.tile([P, CHUNK, PACK], F32, name="term_b")
            nc.vector.tensor_tensor(term_b[:], woven(e2), left[(1, c)], MULT)
            term_a = ring.tile([P, CHUNK, PACK], F32, name="term_a")
            nc.vector.tensor_tensor(term_a[:], woven(e12), left[(0, c)], MULT)
            z = ring.tile([P, CHUNK, PACK], BF16, name="z", align_bytes=64)
            nc.vector.tensor_tensor(z[:], term_a[:], term_b[:], ADD)
            z_q[c] = z

        y_codes = keep.tile([P, V], U32, name="y_codes", align_bytes=64)
        y_scales = keep.tile([P, V], U8, name="y_scales", align_bytes=64)
        out_rows = out_0.rearrange("(p t) v -> p t v", t=PACK)
        out_words = out_1[0].rearrange("p c r -> p (c r)").bitcast(I32)
        y_round = {}

        def last_layer(c):
            z_codes = ring.tile([P, CHUNK], U32, name="z_codes", align_bytes=64)
            z_scales = ring.tile([P, CHUNK], U8, name="z_scales", align_bytes=64)
            quantise(z_q[c][:].rearrange("p v t -> p (v t)"), z_codes[:], z_scales[:])
            bank = product(w3_q, [(z_codes[:], z_scales[:])], "outer", 5)
            y = keep.tile([P, PACK, CHUNK], F32, name="y%d" % c)
            nc.scalar.activation(out=y[:], in_=bank[:], func=RELU)
            queue = nc.scalar if c == CHUNKS - 1 else nc.sync
            queue.dma_start(out_rows[:, :, c * CHUNK : (c + 1) * CHUNK], y[:])
            y_round[c] = (bank, y)

        def planes(c):
            cols = slice(c * CHUNK, (c + 1) * CHUNK)
            bank, y = y_round[c]
            rounded = ring.tile([P, CHUNK, PACK], BF16, name="rounded", align_bytes=64)
            if c < SCALAR_ROUNDS:
                nc.scalar.activation(out=rounded[:], in_=woven(bank), func=RELU)
            else:
                nc.vector.tensor_copy(
                    rounded[:].rearrange("p (u i) t -> p u t i", i=4), y[:].rearrange("p t (u i) -> p u t i", i=4)
                )
            quantise(rounded[:].rearrange("p v t -> p (v t)"), y_codes[:, cols], y_scales[:, cols])
            if c % 2 == 1:
                pair = slice((c - 1) * CHUNK, (c + 1) * CHUNK)
                nc.sync.dma_start(out_words[:, pair], y_codes[:, pair].bitcast(I32))

        w1_grouped = round_weight(w1_raw, "w1")
        gather_words([(1, 0), (0, 0)], "first_words")
        w1_q = quantise_weight(w1_grouped, "w1")
        w2_grouped = round_weight(w2_raw, "w2")
        gather_words([(2, 0), (1, 1), (0, 1)], "w1_grouped")
        w2_q = quantise_weight(w2_grouped, "w2")
        left_products(0)
        gather_words([(2, 1)], "w2_grouped")
        left_products(1)
        interact(0)
        left_products(2)
        w3_grouped = round_weight(w3_raw, "w3")
        w3_q = quantise_weight(w3_grouped, "w3")
        interact(1)
        left_products(3)
        for c in range(CHUNKS):
            last_layer(c)
            if c + 2 < CHUNKS:
                interact(c + 2)
        for c in range(CHUNKS):
            planes(c)
        for q in range(4):
            queue = nc.scalar if q % 2 else nc.sync
            queue.dma_start(
                out_2[0, 4 * q : 4 * q + 4, :].bitcast(I32), y_scales[32 * q : 32 * q + 4, :].bitcast(I32)
            )
